import numpy as np
CORES = [22,46,70,150,174,198,278,302,326,406,430,454]
N = 12
R, W, T = 4096, 128, 256
CAPP = 64
def entries(a): return a.T.reshape(-1)
def pack(v, P): return np.ascontiguousarray(np.asarray(v, np.int32).reshape(-1, P).T)
def lists(rng, how):
    I = rng.integers(0, N * R, (N, T))
    O = np.stack([rng.permutation(np.repeat(np.arange(N), CAPP))[:T] for r in range(N)])
    if how == "full": O = np.stack([rng.permutation(np.repeat(rng.permutation(N)[:T // CAPP], CAPP)) for r in range(N)])
    I = R * O + rng.integers(0, R, (N, T))
    if how == "alike": I = R * O + rng.integers(0, R)
    if how == "edge": I = R * O + np.where(rng.random((N, T)) < 0.5, 0, R - 1)
    if how == "sorted": I = np.sort(I, axis=1)
    return {"idx": np.stack([pack(I[r], 128) for r in range(N)])}
def setup_inputs(rng):
    return dict({"gr": rng.standard_normal((N, T, W), dtype=np.float32)}, **lists(rng, "uniform"))
def setup_inputs_alike(rng):
    d = setup_inputs(rng); d.update(lists(rng, "alike"))
    for k in ("gr",): d[k] = (d[k].astype(np.float32) * 1024.0).astype(d[k].dtype)
    return d
def setup_inputs_edge(rng):
    d = setup_inputs(rng); d.update(lists(rng, "edge"))
    for k in ("gr",): d[k] = (d[k].astype(np.float32) * (1 / 1024.0)).astype(d[k].dtype)
    return d
def setup_inputs_full(rng):
    d = setup_inputs(rng); d.update(lists(rng, "full"))
    return d
def setup_inputs_sorted(rng):
    d = setup_inputs(rng); d.update(lists(rng, "sorted"))
    return d
def check_inputs(x):
    bad = []
    if x["idx"].min() < 0 or x["idx"].max() >= N * R: bad.append("idx out of range")
    if max(int(np.bincount(entries(a) // R, minlength=N).max()) for a in x["idx"]) > CAPP: bad.append("more than CAPP entries of a list point into one rank's part")
    return bad
def reference(gr, idx):
    A = np.zeros((N * R, W))
    for r in range(N):
        np.add.at(A, entries(idx[r]), gr[r].astype(np.float64))
    return {"y": np.stack([A[R * r:R * r + R] for r in range(N)]).astype(np.float32)}

from concourse.bass import DstId, RemoteDMATransfer, IndirectOffsetOnAxis
from concourse.mybir import dt, AluOpType, AxisListType, ActivationFunctionType

NR, CAP, W, ROWS = 12, 64, 128, 4096
WIN = NR * CAP
NCH = NR // 2
ENG = {1: 2, 2: 2, 3: 2, 4: 2, 5: 2, 6: 2, 7: 2, 8: 4, 9: 4, 10: 2, 11: 2}
NOTE = 2
HOP = 2
HALF = ROWS // 2
BIGN = 8192.0
JNK = [sum(WIN - 128 * q for q in range(a)) for a in range(NCH + 1)]

SCRATCH = {
    "iad": ("dram", [NR, 128, 2], "int32"),
    "bkt": ("dram", [WIN, W], "float32"),
    "bk2": ("dram", [NR, 128, CAP], "float32"),
    "lnd": ("dram", [NR, 128, CAP], "float32"),
    "zt": ("sbuf", [128, 1024], "float32"),
    "ii": ("sbuf", [128, 2], "int32"), "di": ("sbuf", [128, 2], "int32"),
    "df": ("sbuf", [128, 2], "float32"),
    "grs": ("sbuf", [128, 256], "float32"),
    "one": ("sbuf", [128, 128], "float32"), "ups": ("sbuf", [128, 128], "float32"),
    "up1": ("sbuf", [128, 128], "float32"), "idn": ("sbuf", [128, 16], "float32"),
    "i64": ("sbuf", [128, 64], "float32"),
    "ohh": ("sbuf", [128, 24], "float16"), "prd": ("sbuf", [128, 24], "float32"),
    "pss": ("sbuf", [128, 2], "float32"), "sli": ("sbuf", [128, 2], "int32"),
    "o16": ("sbuf", [128, 128], "float16"), "u16": ("sbuf", [128, 128], "float16"),
    "lst": ("sbuf", [128, 256], "int32"), "lsf": ("sbuf", [128, 256], "float32"),
    "clp": ("sbuf", [128, 24], "float32"), "mnh": ("sbuf", [128, 24], "float16"),
    "cca": ("sbuf", [128, 24], "float32"), "ccb": ("sbuf", [128, 24], "float32"),
    "ccd": ("sbuf", [128, 24], "float32"), "ccm": ("sbuf", [128, 24], "float32"),
    "pqh": ("sbuf", [128, NR * 128], "float16"),
    "icl": ("sbuf", [128, 8], "float32"), "lpa": ("sbuf", [128, 8], "float32"),
    "tq1": ("sbuf", [128, 8], "float32"), "tq2": ("sbuf", [128, 8], "float32"),
    "tq3": ("sbuf", [128, 8], "float32"), "tq4": ("sbuf", [128, 8], "float32"),
    "cnt": ("sbuf", [128, 8], "float32"),
    "six": ("sbuf", [128, 8], "int32"),
    "jnk": ("sbuf", [128, JNK[NCH]], "float32"),
    "ebf": ("sbuf", [128, NCH * WIN], "float32"),
    "xsb": ("sbuf", [128, WIN], "float32"), "obf": ("sbuf", [128, WIN], "float32"),
    "pr0": ("psum", [128, 512], "float32"), "pr1": ("psum", [128, 512], "float32"),
    "pb0": ("psum", [128, 512], "float32"), "pb1": ("psum", [128, 512], "float32"),
    "po0": ("psum", [128, 512], "float32"), "po1": ("psum", [128, 512], "float32"),
    "po2": ("psum", [128, 512], "float32"), "po3": ("psum", [128, 512], "float32"),
}
SEMAPHORES = ["vs", "ps", "ss", "gs", "ldi", "ldd", "lg0", "lg1", "bz", "zs", "sb", "cp", "ll", "lx", "ls", "ia", "hx",
              "hd", "sc", "da0", "da1", "da2", "da3", "da4", "da5", "xl0", "xl1", "xl2", "xl3", "xl4", "xl5"]


def _plan(T, topo):
    cores = [int(c) for c in T.cores]
    n = len(cores)
    hosts = sorted(set(topo.host(c) for c in cores))
    per = n // len(hosts)
    order = [len([q for q in range(r) if topo.host(cores[q]) == topo.host(cores[r])]) for r in range(n)]

    def far(s, d):
        hs, hd = topo.host(cores[s]), topo.host(cores[d])
        if hs == hd:
            return 0
        if topo.rack(hs) == topo.rack(hd):
            return 1
        return 2 if topo.may_write(cores[s], cores[d]) else 3

    place = [[per * far(s, d) + (order[s] - order[d]) % per for s in range(n)] for d in range(n)]
    owner = [[0] * n for s in range(n)]
    for d in range(n):
        for s in range(n):
            owner[s][place[d][s]] = d
    helper = {}
    for s in range(n):
        ends = [cores[d] for d in range(n) if far(s, d) == 3]
        twin = [cores[x] for x in range(n) if far(s, x) == 2 and topo.chip(cores[x]) == topo.chip(cores[s])][0]
        helper[s] = [c for c in range(max(0, twin - 16), twin + 17)
                     if c not in cores and topo.host(c) == topo.host(twin) and topo.chip(c) == topo.chip(twin)
                     and topo.die(c) == topo.die(twin) and topo.may_write(cores[s], c)
                     and all(topo.may_write(c, e) for e in ends)][0]
    return cores, owner, helper, per


def _masks(topo, src, dsts, sizes):
    m = topo.mask(src, dsts[0])
    for d in dsts:
        m &= topo.mask(src, d)
    bits = [1 << e for e in range(16) if (m >> e) & 1]
    out, at = [], 0
    for k in sizes:
        out.append(sum(bits[at:at + k]))
        at += k
    return out


def rank_program(g, core, T, topo):
    cores, owner, helper, per = _plan(T, topo)
    S = T.sem
    A = AluOpType
    r = T.rank_of(core)

    def to(e):
        rid, pid = topo.addr(e, core)
        return DstId(rid=rid, pnc=pid)

    def note(src, ends, slots, sem, mask):
        return RemoteDMATransfer(dst_ids=[to(e) for e in ends], dma_engine_mask=mask, remote_sem=sem, srcs=[src],
                                 dsts=[T.iad[q] for q in slots])

    def send(items):
        ms = _masks(topo, core, [i[0] for i in items], [i[1] for i in items])
        g.remote_dma_fused([RemoteDMATransfer(dst_ids=[to(i[0])], dma_engine_mask=ms[k], remote_sem=i[2], src=i[3],
                                              dst=T.lnd[i[4]]) for k, i in enumerate(items)], local_sem=S.ls)
        return sum(i[1] for i in items)

    DIAG = [NR - 1 - b for b in range(per)]
    UP = sorted(DIAG)

    if r is None:
        frm = [s for s in helper if helper[s] == core]
        if not frm:
            return
        s = frm[0]
        ends = [cores[owner[s][pl]] for pl in DIAG]
        g.wait_ge(S.hx, NOTE)
        g.remote_dma_fused([note(T.iad[1], ends, DIAG, S.ia, _masks(topo, core, ends, [NOTE])[0])], local_sem=S.ls)
        g.wait_ge(S.hd, HOP * per)
        out = send([(cores[owner[s][pl]], ENG[pl], S["da%d" % (pl // 2)], T.lnd[pl], pl) for pl in UP])
        g.wait_ge(S.ls, NOTE + out)
        return

    v, pe, sc, sy = g.vector, g.tensor, g.scalar, g.sync
    Q = {"v": v, "p": pe, "s": sc, "y": sy, "g": g}
    OWNSEM = {"v": "vs", "p": "ps", "s": "ss", "g": "gs"}
    tot, seen = {}, {}
    COPY = ActivationFunctionType.Copy

    def op(q, ins):
        sem = OWNSEM[q]
        ins.then_inc(S[sem], 1)
        tot[sem] = tot.get(sem, 0) + 1
        return (sem, tot[sem])

    def dm(ins, sem):
        ins.then_inc(S[sem], 16)
        tot[sem] = tot.get(sem, 0) + 16
        return (sem, tot[sem])

    def need(q, *toks):
        for sem, val in toks:
            if seen.get((q, sem), 0) < val:
                Q[q].wait_ge(S[sem], val)
                seen[(q, sem)] = val

    def ts(out, in0, s1, op0, s2=None, op1=None):
        if op1 is None:
            return v.tensor_scalar(out=out, in0=in0, scalar1=s1, scalar2=None, op0=op0)
        return v.tensor_scalar(out=out, in0=in0, scalar1=s1, scalar2=s2, op0=op0, op1=op1)

    t_ldd = dm(sy.dma_start(T.iad[0], T.idx[:, :]), "ldd")
    t_ldi = dm(sy.dma_start(T.ii[:, :], T.idx[:, :]), "ldi")
    t_g0 = dm(sc.dma_start(T.grs[:, 0:128], T.gr[0:128, :]), "lg0")
    v_one = op("v", v.memset(T.one[:, :], 1.0))
    v_z0 = op("v", v.memset(T.zt[:, 0:WIN], 0.0))
    need("v", v_one)
    v_o16 = op("v", v.tensor_copy(out=T.o16[:, :], in_=T.one[:, :]))
    v_z1 = op("v", v.memset(T.zt[:, WIN:1024], 0.0))
    need("y", v_z0)
    t_bz = dm(sy.dma_start(T.bkt[:, :], T.zt[:, 0:WIN]), "bz")

    need("g", v_one)
    g_ups = op("g", g.affine_select(T.ups[:, :], T.one[:, :], [[1, 128]], A.is_gt, 0.0, 0, -1))
    g_i64 = op("g", g.iota(T.i64[:, :], [[1, CAP]], 0, 0, allow_small_or_imprecise_dtypes=True))
    need("g", t_ldd)
    groups = [[pl for pl in range(per * f, per * f + per) if pl] for f in range(3)]
    allends = [helper[r]] + [cores[owner[r][pl]] for grp in groups for pl in grp]
    ms = _masks(topo, core, allends, [NOTE] * 4)
    g.remote_dma_fused([note(T.iad[0], [helper[r]], [1], S.hx, ms[0])] +
                       [note(T.iad[0], [cores[owner[r][pl]] for pl in groups[f]], groups[f], S.ia, ms[1 + f])
                        for f in range(3)], local_sem=S.lx)
    t_lx = ("lx", 4 * NOTE)
    t_g1 = dm(g.dma_start(T.grs[:, 128:256], T.gr[128:256, :]), "lg1")
    g_idn = op("g", g.affine_select(T.idn[0:NR, 0:NR], T.one[0:NR, 0:NR], [[1, NR]], A.is_equal, 0.0, 0, -1))
    g_up1 = op("g", g.affine_select(T.up1[:, :], T.one[:, :], [[1, 128]], A.is_ge, 0.0, 0, -1))

    need("v", g_ups)
    v_u16 = op("v", v.tensor_copy(out=T.u16[:, :], in_=T.ups[:, :]))
    need("v", t_ldi)
    x = op("v", ts(T.di[:, :], T.ii[:, :], 12, A.arith_shift_right))
    need("v", x)
    x = op("v", v.tensor_copy(out=T.df[:, :], in_=T.di[:, :]))
    need("v", x, g_i64)
    for b in range(2):
        v_oh = op("v", ts(T.ohh[:, 12 * b:12 * b + 12], T.i64[:, 0:NR], T.df[:, b:b + 1], A.is_equal))
    need("p", v_oh)
    op("p", pe.matmul(T.pr0[:, 0:12], T.u16[:, :], T.ohh[:, 0:12], True, True))
    pe.matmul(T.pr0[:, 12:24], T.u16[:, :], T.ohh[:, 12:24], True, False)
    p_cnt = op("p", pe.matmul(T.pr0[:, 12:24], T.o16[:, :], T.ohh[:, 0:12], False, True))
    need("v", v_oh, p_cnt)
    x = op("v", v.tensor_tensor(out=T.prd[:, :], in0=T.ohh[:, :], in1=T.pr0[:, 0:24], op=A.mult))
    need("v", x)
    for b in range(2):
        x = op("v", v.tensor_reduce(out=T.pss[:, b:b + 1], in_=T.prd[:, 12 * b:12 * b + 12], axis=AxisListType.X, op=A.add))
    need("v", x)
    v_sl = [op("v", ts(T.sli[:, b:b + 1], T.df[:, b:b + 1], float(CAP), A.mult, T.pss[:, b:b + 1], A.add))
            for b in range(2)]

    for b in range(2):
        need("g", v_sl[b], t_bz, (t_g0, t_g1)[b])
        t_sb = dm(g.indirect_dma_start(T.bkt[:], IndirectOffsetOnAxis(ap=T.sli[:, b:b + 1], axis=0),
                                       T.grs[:, 128 * b:128 * b + 128], None, bounds_check=WIN - 1), "sb")

    need("y", t_lx, v_z1)
    for q in range(4):
        t_zs = dm(sy.dma_start(T.y[1024 * q:1024 * q + 1024, :], T.zt[:, :]), "zs")
    need("y", t_sb)
    t_cp = dm(sy.dma_start(T.bk2[:, :, :], T.bkt[:, :]), "cp")
    dm(sy.dma_start(T.xsb[0:CAP, 0:128], T.bkt[CAP * r:CAP * r + CAP, :]), "xl0")

    def mine(pl):
        return (cores[owner[r][pl]], ENG[pl], S["da%d" % (pl // 2)], T.bk2[owner[r][pl]], pl)

    need("g", t_cp)
    sent = send([(helper[r], HOP, S.hd, T.bk2[owner[r][pl]], pl) for pl in UP] + [mine(1)])
    sent += send([mine(2), mine(3), mine(4), mine(5)])
    sent += send([mine(6), mine(7), mine(8)])

    got = [sum(ENG[pl] for pl in (2 * k, 2 * k + 1) if pl) for k in range(NCH)]
    t_x = [None] * NCH
    need("y", ("da0", got[0]))
    t_x[0] = dm(sy.dma_start(T.xsb[CAP:128, 0:128], T.lnd[1]), "xl0")
    for k in range(1, NCH):
        need("y", ("da%d" % k, got[k]))
        t_x[k] = dm(sy.dma_start(T.xsb[:, 128 * k:128 * k + 128], T.lnd[2 * k:2 * k + 2, :, :]), "xl%d" % k)

    need("s", ("ia", NOTE * (NR - 1)), t_ldd)
    t_ll = dm(sc.dma_start(T.lst[0:NR, :], T.iad[:, :, :]), "ll")
    need("v", t_ll)
    for b in range(2):
        v_ls = op("v", v.tensor_copy(out=T.lsf[0:NR, 128 * b:128 * b + 128], in_=T.lst[0:NR, b:256:2]))
    need("p", v_ls, g_idn)
    for b in range(2):
        p_ia = op("p", pe.matmul(T.pr1[:, 12 * b:12 * b + 12], T.lsf[0:NR, 128 * b:128 * b + 128], T.idn[0:NR, 0:NR],
                                 True, True))
    base = float(ROWS * r)
    need("v", p_ia)
    x = op("v", ts(T.clp[:, :], T.pr1[:, 0:24], base + ROWS - 1, A.min, base, A.max))
    need("v", x)
    v_mn = op("v", v.tensor_tensor(out=T.mnh[:, :], in0=T.clp[:, :], in1=T.pr1[:, 0:24], op=A.is_equal))
    need("p", v_mn)
    op("p", pe.matmul(T.pr0[:, 0:12], T.u16[:, :], T.mnh[:, 0:12], True, True))
    pe.matmul(T.pr0[:, 12:24], T.u16[:, :], T.mnh[:, 12:24], True, False)
    p_pos = op("p", pe.matmul(T.pr0[:, 12:24], T.o16[:, :], T.mnh[:, 0:12], False, True))
    op("v", ts(T.cca[:, :], T.pr1[:, 0:24], base + HALF - 1, A.subtract, 0.0, A.max))
    x = op("v", ts(T.ccb[:, :], T.pr1[:, 0:24], base + HALF, A.subtract, 0.0, A.min))
    need("v", x)
    x = op("v", v.tensor_tensor(out=T.ccd[:, :], in0=T.cca[:, :], in1=T.ccb[:, :], op=A.add))
    need("v", x)
    x = op("v", v.tensor_tensor(out=T.ccm[:, :], in0=T.ccd[:, :], in1=T.mnh[:, :], op=A.mult))
    need("v", x, p_pos)
    pb = [T.pb0, T.pb0, T.pb0, T.pb0, T.pb1, T.pb1]
    for k in range(NCH):
        for b in range(2):
            for h in range(2):
                col = 12 * b + 2 * k + h
                q0 = 128 * (2 * k + b) + CAP * h
                v_pq = op("v", ts(T.pqh[:, q0:q0 + CAP], T.i64[:, :], T.pr0[:, col:col + 1], A.is_equal,
                                  T.ccm[:, col:col + 1], A.mult))
        need("p", v_pq)
        q0 = 256 * k
        c0 = 128 * (k % 4)
        pe.matmul(pb[k][:, c0:c0 + 128], T.o16[:, :], T.pqh[:, q0:q0 + 128], True, False)
        op("p", pe.matmul(pb[k][:, c0:c0 + 128], T.o16[:, :], T.pqh[:, q0 + 128:q0 + 256], False, True))
        pe.matmul(T.pr1[:, 32 + k:33 + k], T.pqh[:, q0:q0 + 128], T.o16[:, 0:1], True, False)
        p_ic = op("p", pe.matmul(T.pr1[:, 32 + k:33 + k], T.pqh[:, q0 + 128:q0 + 256], T.o16[:, 0:1], False, True))
    need("v", p_ic)
    v_icl = op("v", v.tensor_copy(out=T.icl[:, 0:NCH], in_=T.pr1[:, 32:32 + NCH]))
    need("v", v_icl, g_up1)

    po = [T.po0, T.po1, T.po2, T.po3, T.pr0, T.pr1]
    c_o, c_n, v_m, v_six, p_o = [0] * NCH, [0] * NCH, [0] * NCH, [0] * NCH, [0] * NCH

    def cols(lo, hi):
        out = []
        if lo < 512:
            out.append((lo, min(hi, 512), T.pb0, 0))
        if hi > 512:
            out.append((max(lo, 512), hi, T.pb1, 512))
        return [o for o in out if o[0] < o[1]]

    def cmpr(a):
        lo, e0 = 128 * a, WIN * a
        d = None
        for c0, c1, bank, off in cols(lo, lo + 128):
            d = op("v", ts(T.ebf[:, e0 + c0:e0 + c1], bank[:, c0 - off:c1 - off], T.icl[:, a:a + 1], A.is_equal))
        for c0, c1, bank, off in cols(lo + 128, WIN):
            op("v", ts(T.ebf[:, e0 + c0:e0 + c1], bank[:, c0 - off:c1 - off], T.icl[:, a:a + 1], A.is_equal))
        need("v", d)
        v_m[a] = op("v", v.tensor_tensor(out=T.ebf[:, e0 + lo:e0 + lo + 128], in0=T.ebf[:, e0 + lo:e0 + lo + 128],
                                         in1=T.up1[:, :], op=A.mult))

    def count(a):
        lo, e0 = 128 * a, WIN * a
        need("s", v_m[a])
        c_n[a] = op("s", sc.activation(out=T.jnk[:, JNK[a]:JNK[a + 1]], in_=T.ebf[:, e0 + lo:e0 + WIN], func=COPY,
                                       accum_out=T.cnt[:, a:a + 1]))

    def last(a):
        need("v", c_n[a], v_lpa)
        v_six[a] = op("v", ts(T.six[:, a:a + 1], T.cnt[:, a:a + 1], -BIGN, A.mult, T.lpa[:, a:a + 1], A.add))

    def sums(k, a0, a1):
        need("p", v_m[k])
        mm = None
        for a in range(a0, a1):
            need("p", t_x[a])
            mm = pe.matmul(po[k][:, 0:128], T.ebf[:, WIN * a + 128 * k:WIN * a + 128 * k + 128],
                           T.xsb[:, 128 * a:128 * a + 128], a == 0, a == k)
        if a1 == k + 1:
            p_o[k] = op("p", mm)

    def evac(k):
        need("s", p_o[k])
        c_o[k] = op("s", sc.activation(out=T.obf[:, 128 * k:128 * k + 128], in_=po[k][:, 0:128], func=COPY))

    cmpr(0)
    op("v", ts(T.tq1[:, 0:NCH], T.icl[:, 0:NCH], 0.0, A.is_gt, -1.0, A.mult))
    op("v", ts(T.tq2[:, 0:NCH], T.icl[:, 0:NCH], 0.0, A.is_equal, -65536.0, A.mult))
    x = op("v", ts(T.tq4[:, 0:NCH], T.icl[:, 0:NCH], float(HALF) + BIGN, A.add))
    need("v", x)
    x = op("v", v.tensor_tensor(out=T.tq3[:, 0:NCH], in0=T.tq1[:, 0:NCH], in1=T.tq2[:, 0:NCH], op=A.add))
    need("v", x)
    v_lpa = op("v", v.tensor_tensor(out=T.lpa[:, 0:NCH], in0=T.tq3[:, 0:NCH], in1=T.tq4[:, 0:NCH], op=A.add))
    count(0)
    sums(0, 0, 1)
    evac(0)
    for a in range(1, 4):
        cmpr(a)
        last(a - 1)
        count(a)
        sums(a, 0, a + 1)
        evac(a)
    cmpr(4)
    cmpr(5)
    last(3)
    count(4)
    count(5)
    last(4)
    last(5)
    sums(4, 0, 4)
    sums(5, 0, 4)
    sums(4, 4, 5)
    evac(4)
    sums(5, 4, 6)
    evac(5)

    need("g", t_zs)
    for k in range(NCH):
        need("g", v_six[k], c_o[k])
        dm(g.indirect_dma_start(T.y[:], IndirectOffsetOnAxis(ap=T.six[:, k:k + 1], axis=0),
                                T.obf[:, 128 * k:128 * k + 128], None,
                                bounds_check=ROWS - 1, oob_is_err=False), "sc")
    tot["lx"] = 4 * NOTE
    tot["ls"] = sent
    tot["ia"] = NOTE * (NR - 1)
    for k in range(NCH):
        tot["da%d" % k] = got[k]
    for sem in sorted(tot):
        need("g", (sem, tot[sem]))
